import numpy as np
import ml_dtypes


def mxq(x, axis, fmt="e4m3"):
    dtype, down = {"e4m3": (ml_dtypes.float8_e4m3fn, 7), "e5m2": (ml_dtypes.float8_e5m2, 14)}[fmt]
    v = np.moveaxis(np.asarray(x, np.float32).astype(ml_dtypes.bfloat16).astype(np.float64), axis, -1)
    blocks = v.reshape(v.shape[:-1] + (-1, 32))
    amax = np.abs(blocks).max(-1, keepdims=True)
    byte = np.maximum(np.where(amax > 0, np.frexp(amax)[1] - 1 + 127, 0) - down, 1)
    scale = np.exp2(byte - 127.0)
    codes = (blocks / scale).astype(np.float32).astype(dtype).astype(np.float64)
    return np.moveaxis((codes * scale).reshape(v.shape), -1, axis)


WIDE = False


def mx_kscale(k):
    if not WIDE:
        return np.ones(k)
    levels = np.array([10, -10, 5, -5, 0])
    if k % 512:
        return np.exp2(np.random.permutation(np.resize(levels, k // 32))).repeat(32)
    a = np.empty((k // 512, 16))
    for p in range(k // 512):
        a[p, :8] = np.random.permutation(np.resize(levels, 8))
        for g in range(8):
            far = levels[np.abs(levels - a[p, g]) >= 10]
            a[p, g + 8] = far[np.random.randint(len(far))]
    return np.exp2(a.ravel()).repeat(32)


def f64(x):
    return np.asarray(x).astype(np.float64)


def striped(idx):
    return np.tile(idx.reshape(-1, 16).T, (8, 1)).astype(np.uint16)


def unstriped(offs):
    return offs[:16].T.reshape(-1).astype(np.int64)


def relu(v):
    return np.maximum(v, 0.0)


K, T, S, H, N, U = 512, 2048, 1024, 512, 128, 1024


def setup_inputs():
    n = np.random.standard_normal
    s = mx_kscale(K)[:, None]
    u = mx_kscale(H)
    return {
        "xT": (n((K, T)) * s).astype(np.float32),
        "w1": (n((K, H)) / np.sqrt(2 * K) / s * u).astype(np.float32),
        "w2": (n((K, H)) / np.sqrt(2 * K) / s * u).astype(np.float32),
        "w3": (n((H, N)) / np.sqrt(H) / u[:, None]).astype(np.float32),
        "offs": striped(np.random.permutation(T)[:S]),
        "src": striped(np.random.permutation(S)[(S * np.random.uniform(0, 1, U) ** 4).astype(np.int64)]),
        "dst": striped(np.random.permutation(S)),
    }


def reference(xT, w1, w2, w3, offs, src, dst):
    xq = mxq(f64(xT)[:, unstriped(offs)], 0, "e4m3")
    y = mxq(f64(w1), 0, "e4m3").T @ xq
    e = mxq(f64(w2), 0, "e4m3").T @ xq
    z = relu(y[:, unstriped(src)] + e[:, unstriped(dst)])
    return mxq(f64(w3), 0, "e4m3").T @ mxq(z, 0, "e4m3")

@@ -1,0 +1,199 @@
+from contextlib import ExitStack
+
+import concourse.mybir as mybir
+
+K, T, S, H, N, U = 512, 2048, 1024, 512, 128, 1024
+FLOPS = 2 * (2 * K * H * S + H * N * U)
+
+F32 = mybir.dt.float32
+BF16 = mybir.dt.bfloat16
+U32 = mybir.dt.uint32
+U16 = mybir.dt.uint16
+U8 = mybir.dt.uint8
+FP8X4 = mybir.dt.float8_e4m3fn_x4
+COPY = mybir.ActivationFunctionType.Copy
+RELU = mybir.ActivationFunctionType.Relu
+ADD = mybir.AluOpType.add
+
+P = 128
+PACK = 4
+HALF = 512
+LIST_ROWS = 16
+NODE_CHUNKS = ((512, 512, 512, 512), (512, 512, 512, 256, 256))
+W_CHUNK = 128
+SCALAR_CHUNKS = 2
+PICK_CHUNKS = (512, 256, 256)
+EDGE_CHUNKS = (256, 256, 256, 128, 128)
+
+
+def list_slice(tile, start, count):
+    return tile[:, start // LIST_ROWS : (start + count) // LIST_ROWS]
+
+
+def tile_picked_hub_relu_e_kernel(tc, xT, w1, w2, w3, offs, src, dst, out):
+    nc = tc.nc
+    with ExitStack() as ctx:
+        keep = ctx.enter_context(tc.tile_pool(name="keep", bufs=1))
+        ring = ctx.enter_context(tc.tile_pool(name="ring", bufs=3))
+        psum = ctx.enter_context(tc.psum_pool(name="psum", bufs=1))
+
+        offs_sb = keep.tile([P, S // LIST_ROWS], U16, name="offs_sb")
+        src_sb = keep.tile([P, U // LIST_ROWS], U16, name="src_sb")
+        dst_sb = keep.tile([P, U // LIST_ROWS], U16, name="dst_sb")
+
+        x_rows = xT.rearrange("(p j) t -> p j t", j=PACK)
+        x_raw = {}
+        for u in range(2):
+            c0 = 0
+            for c, width in enumerate(NODE_CHUNKS[u]):
+                raw = keep.tile([P, 2, width], F32, name=f"x_raw{u}_{c}")
+                nc.sync.dma_start(out=raw[:], in_=x_rows[:, 2 * u : 2 * u + 2, c0 : c0 + width])
+                x_raw[u, c] = (raw, c0, width)
+                c0 = c0 + width
+                if (u, c) == (0, 1):
+                    nc.sync.dma_start(offs_sb[:], offs)
+
+        def load_weight(w, name):
+            rows = w.rearrange("(p j) c -> p j c", j=PACK)
+            raws = []
+            for q in range(w.shape[1] // W_CHUNK):
+                raw = keep.tile([P, PACK, W_CHUNK], F32, name=f"{name}_raw{q}")
+                nc.sync.dma_start(out=raw[:], in_=rows[:, :, q * W_CHUNK : (q + 1) * W_CHUNK])
+                raws.append(raw)
+            return raws
+
+        w1_raw = load_weight(w1, "w1")
+        nc.sync.dma_start(src_sb[:], src)
+        w2_raw = load_weight(w2, "w2")
+        nc.sync.dma_start(dst_sb[:], dst)
+        w3_raw = load_weight(w3, "w3")
+
+        def quantize(grouped, width, name, pool):
+            codes = pool.tile([P, width], U32, name=f"{name}_codes", align_bytes=64)
+            scales = pool.tile([P, width], U8, name=f"{name}_scales", align_bytes=64)
+            nc.vector.quantize_mx(out=codes[:].bitcast(FP8X4), scales=scales[:], in_=grouped)
+            return codes, scales
+
+        def deal_weight(raws, name):
+            grouped = keep.tile([P, PACK, P, PACK], BF16, name=f"{name}_grouped", align_bytes=64)
+            per = W_CHUNK // PACK
+            for q, raw in enumerate(raws):
+                nc.scalar.copy(
+                    out=grouped[:, :, q * per : (q + 1) * per, :].rearrange("p t m j -> p m t j"),
+                    in_=raw[:].rearrange("p j (m t) -> p m t j", t=PACK),
+                )
+            return grouped
+
+        pick_starts = [sum(PICK_CHUNKS[:h]) for h in range(len(PICK_CHUNKS))]
+        picked = [keep.tile([P, width, PACK], BF16, name=f"picked{h}", align_bytes=64) for h, width in enumerate(PICK_CHUNKS)]
+
+        def cast_pairs(u):
+            pairs = keep.tile([P, T, 2], BF16, name=f"pairs{u}", align_bytes=64)
+            last = len(NODE_CHUNKS[u]) - 1
+            for c in range(last + 1):
+                raw, c0, width = x_raw[u, c]
+                dst_ap = pairs[:, c0 : c0 + width, :]
+                src_ap = raw[:].rearrange("p e c -> p c e")
+                if u == 0 or c >= SCALAR_CHUNKS:
+                    nc.vector.tensor_copy(out=dst_ap, in_=src_ap)
+                else:
+                    nc.scalar.activation(dst_ap, src_ap, COPY)
+            return pairs[:].rearrange("p t e -> p (t e)").bitcast(U32)
+
+        def gather_pairs(words, u, h):
+            target = picked[h][:].rearrange("p n j -> p (n j)").bitcast(U32).rearrange("p (n u) -> p n u", u=2)
+            nc.vector.tensor_copy(out=target[:, :, u], in_=words.indirect(list_slice(offs_sb, pick_starts[h], PICK_CHUNKS[h])))
+
+        def quantize_picked(h):
+            return quantize(picked[h][:].rearrange("p n j -> p (n j)"), PICK_CHUNKS[h], f"x{h}", keep)
+
+        def quantize_w1(t):
+            return quantize(w1_grouped[:, t, :, :].rearrange("p m j -> p (m j)"), P, f"w1_{t}", keep)
+
+        words0 = cast_pairs(0)
+        for h in range(len(PICK_CHUNKS)):
+            gather_pairs(words0, 0, h)
+        words1 = cast_pairs(1)
+        w1_grouped = deal_weight(w1_raw, "w1")
+        gather_pairs(words1, 1, 0)
+        gather_pairs(words1, 1, 1)
+        x_mx = [quantize_picked(0)]
+        gather_pairs(words1, 1, 2)
+        x_mx.append(quantize_picked(1))
+        w1_mx = [quantize_w1(0)]
+        x_mx.append(quantize_picked(2))
+        w1_mx.extend([quantize_w1(t) for t in range(1, PACK)])
+
+        def node_product(w_codes, w_scales, name):
+            result = keep.tile([P, S], F32, name=name)
+            for h, width in enumerate(PICK_CHUNKS):
+                acc = psum.tile([P, width], F32, name="acc", bufs=6)
+                nc.tensor.matmul_mx(
+                    out=acc[:],
+                    lhsT=w_codes.bitcast(FP8X4),
+                    lhsT_scale=w_scales,
+                    rhs=x_mx[h][0][:].bitcast(FP8X4),
+                    rhs_scale=x_mx[h][1][:],
+                    start=True,
+                    stop=True,
+                )
+                nc.scalar.copy(out=result[:, pick_starts[h] : pick_starts[h] + width], in_=acc[:])
+            return result
+
+        y = [node_product(w1_mx[t][0][:], w1_mx[t][1][:], f"y{t}") for t in range(PACK)]
+        w2_grouped = deal_weight(w2_raw, "w2")
+
+        y_src = [keep.tile([P, U], F32, name=f"y_src{t}") for t in range(PACK)]
+
+        def gather_sources(t):
+            for h in range(2):
+                nc.vector.tensor_copy(
+                    out=y_src[t][:, h * HALF : (h + 1) * HALF],
+                    in_=y[t][:].indirect(list_slice(src_sb, h * HALF, HALF)),
+                )
+
+        gather_sources(0)
+        gather_sources(1)
+        w2_codes, w2_scales = quantize(w2_grouped[:].rearrange("p t m j -> p (t m j)"), H, "w2", keep)
+        e = [node_product(w2_codes[:, t * P : (t + 1) * P], w2_scales[:, t * P : (t + 1) * P], f"e{t}") for t in range(PACK)]
+        w3_grouped = keep.tile([P, N, PACK], BF16, name="w3_grouped", align_bytes=64)
+        nc.scalar.copy(out=w3_grouped[:], in_=w3_raw[0][:].rearrange("p j c -> p c j"))
+        gather_sources(2)
+        gather_sources(3)
+        w3_codes, w3_scales = quantize(w3_grouped[:].rearrange("p c j -> p (c j)"), N, "w3", keep)
+
+        def edge_sums(r0, width):
+            sums = ring.tile([P, PACK, width], F32, name="sums")
+            for t in range(PACK):
+                nc.vector.tensor_tensor(
+                    sums[:, t, :], e[t][:].indirect(list_slice(dst_sb, r0, width)), y_src[t][:, r0 : r0 + width], ADD
+                )
+            z = ring.tile([P, width, PACK], BF16, name="z", align_bytes=64)
+            nc.scalar.activation(z[:], sums[:].rearrange("p t r -> p r t"), RELU)
+            return z
+
+        def edge_outputs(z, r0, width):
+            z_codes, z_scales = quantize(z[:].rearrange("p r t -> p (r t)"), width, "z", ring)
+            acc = psum.tile([P, width], F32, name="out_acc", bufs=2)
+            nc.tensor.matmul_mx(
+                out=acc[:],
+                lhsT=w3_codes[:].bitcast(FP8X4),
+                lhsT_scale=w3_scales[:],
+                rhs=z_codes[:].bitcast(FP8X4),
+                rhs_scale=z_scales[:],
+                start=True,
+                stop=True,
+            )
+            result = ring.tile([P, width], F32, name="result")
+            nc.scalar.copy(out=result[:], in_=acc[:])
+            nc.sync.dma_start(out=out[:, r0 : r0 + width], in_=result[:])
+
+        pending = None
+        r0 = 0
+        for width in EDGE_CHUNKS:
+            z = edge_sums(r0, width)
+            if pending is not None:
+                edge_outputs(*pending)
+            pending = (z, r0, width)
+            r0 = r0 + width
+        edge_outputs(*pending)

@@ -18,12 +18,12 @@ ADD = mybir.AluOpType.add
 P = 128
 PACK = 4
 HALF = 512
+QUARTER = 256
 LIST_ROWS = 16
-NODE_CHUNKS = ((512, 512, 512, 512), (512, 512, 512, 256, 256))
-W_CHUNK = 128
-SCALAR_CHUNKS = 2
-PICK_CHUNKS = (512, 256, 256)
+NODE_CHUNKS = ((1024, 512, 512), (512, 512, 512, 256, 256))
+SCALAR_CHUNKS = 3
 EDGE_CHUNKS = (256, 256, 256, 128, 128)
+PINNED_CHUNKS = 2
 
 
 def list_slice(tile, start, count):
@@ -34,7 +34,6 @@ def tile_picked_hub_relu_e_kernel(tc, xT, w1, w2, w3, offs, src, dst, out):
     nc = tc.nc
     with ExitStack() as ctx:
         keep = ctx.enter_context(tc.tile_pool(name="keep", bufs=1))
-        ring = ctx.enter_context(tc.tile_pool(name="ring", bufs=3))
         psum = ctx.enter_context(tc.psum_pool(name="psum", bufs=1))
 
         offs_sb = keep.tile([P, S // LIST_ROWS], U16, name="offs_sb")
@@ -50,150 +49,161 @@ def tile_picked_hub_relu_e_kernel(tc, xT, w1, w2, w3, offs, src, dst, out):
                 nc.sync.dma_start(out=raw[:], in_=x_rows[:, 2 * u : 2 * u + 2, c0 : c0 + width])
                 x_raw[u, c] = (raw, c0, width)
                 c0 = c0 + width
-                if (u, c) == (0, 1):
+                if (u, c) == (0, 0):
                     nc.sync.dma_start(offs_sb[:], offs)
 
-        def load_weight(w, name):
-            rows = w.rearrange("(p j) c -> p j c", j=PACK)
-            raws = []
-            for q in range(w.shape[1] // W_CHUNK):
-                raw = keep.tile([P, PACK, W_CHUNK], F32, name=f"{name}_raw{q}")
-                nc.sync.dma_start(out=raw[:], in_=rows[:, :, q * W_CHUNK : (q + 1) * W_CHUNK])
-                raws.append(raw)
-            return raws
-
-        w1_raw = load_weight(w1, "w1")
+        w1_rows = w1.rearrange("(p j) c -> p j c", j=PACK)
+        w1_raw = []
+        for q in range(2):
+            raw = keep.tile([P, PACK, H // 2], F32, name=f"w1_raw{q}")
+            nc.sync.dma_start(out=raw[:], in_=w1_rows[:, :, q * (H // 2) : (q + 1) * (H // 2)])
+            w1_raw.append(raw)
         nc.sync.dma_start(src_sb[:], src)
-        w2_raw = load_weight(w2, "w2")
+        w2_raw = keep.tile([P, PACK, H], F32, name="w2_raw")
+        nc.sync.dma_start(out=w2_raw[:], in_=w2.rearrange("(p j) c -> p j c", j=PACK))
         nc.sync.dma_start(dst_sb[:], dst)
-        w3_raw = load_weight(w3, "w3")
+        w3_raw = keep.tile([P, PACK, N], F32, name="w3_raw")
+        nc.sync.dma_start(out=w3_raw[:], in_=w3.rearrange("(p j) c -> p j c", j=PACK))
 
-        def quantize(grouped, width, name, pool):
-            codes = pool.tile([P, width], U32, name=f"{name}_codes", align_bytes=64)
-            scales = pool.tile([P, width], U8, name=f"{name}_scales", align_bytes=64)
-            nc.vector.quantize_mx(out=codes[:].bitcast(FP8X4), scales=scales[:], in_=grouped)
+        def mx_tiles(width, name, tag=""):
+            codes = keep.tile([P, width], U32, name=f"{name}_codes", tag=tag, align_bytes=64)
+            scales = keep.tile([P, width], U8, name=f"{name}_scales", align_bytes=64)
             return codes, scales
 
-        def deal_weight(raws, name):
-            grouped = keep.tile([P, PACK, P, PACK], BF16, name=f"{name}_grouped", align_bytes=64)
-            per = W_CHUNK // PACK
-            for q, raw in enumerate(raws):
-                nc.scalar.copy(
-                    out=grouped[:, :, q * per : (q + 1) * per, :].rearrange("p t m j -> p m t j"),
-                    in_=raw[:].rearrange("p j (m t) -> p m t j", t=PACK),
-                )
-            return grouped
+        def quantize(mx, start, width, grouped):
+            codes, scales = mx
+            nc.vector.quantize_mx(
+                out=codes[:, start : start + width].bitcast(FP8X4), scales=scales[:, start : start + width], in_=grouped
+            )
 
-        pick_starts = [sum(PICK_CHUNKS[:h]) for h in range(len(PICK_CHUNKS))]
-        picked = [keep.tile([P, width, PACK], BF16, name=f"picked{h}", align_bytes=64) for h, width in enumerate(PICK_CHUNKS)]
+        def product(acc, stationary, m0, moving, n0, width):
+            nc.tensor.matmul_mx(
+                out=acc[:],
+                lhsT=stationary[0][:, m0 : m0 + P].bitcast(FP8X4),
+                lhsT_scale=stationary[1][:, m0 : m0 + P],
+                rhs=moving[0][:, n0 : n0 + width].bitcast(FP8X4),
+                rhs_scale=moving[1][:, n0 : n0 + width],
+                start=True,
+                stop=True,
+            )
+
+        pieces = ((0, HALF), (HALF, QUARTER), (HALF + QUARTER, QUARTER))
+        picked = [keep.tile([P, width, PACK], BF16, name=f"picked{h}", align_bytes=64) for h, (s0, width) in enumerate(pieces)]
 
         def cast_pairs(u):
             pairs = keep.tile([P, T, 2], BF16, name=f"pairs{u}", align_bytes=64)
-            last = len(NODE_CHUNKS[u]) - 1
-            for c in range(last + 1):
+            for c in range(len(NODE_CHUNKS[u])):
                 raw, c0, width = x_raw[u, c]
-                dst_ap = pairs[:, c0 : c0 + width, :]
-                src_ap = raw[:].rearrange("p e c -> p c e")
-                if u == 0 or c >= SCALAR_CHUNKS:
-                    nc.vector.tensor_copy(out=dst_ap, in_=src_ap)
+                rounded = pairs[:, c0 : c0 + width, :]
+                values = raw[:].rearrange("p e c -> p c e")
+                if u == 1 and c < SCALAR_CHUNKS:
+                    nc.scalar.activation(rounded, values, COPY)
                 else:
-                    nc.scalar.activation(dst_ap, src_ap, COPY)
+                    nc.vector.tensor_copy(out=rounded, in_=values)
             return pairs[:].rearrange("p t e -> p (t e)").bitcast(U32)
 
         def gather_pairs(words, u, h):
             target = picked[h][:].rearrange("p n j -> p (n j)").bitcast(U32).rearrange("p (n u) -> p n u", u=2)
-            nc.vector.tensor_copy(out=target[:, :, u], in_=words.indirect(list_slice(offs_sb, pick_starts[h], PICK_CHUNKS[h])))
-
-        def quantize_picked(h):
-            return quantize(picked[h][:].rearrange("p n j -> p (n j)"), PICK_CHUNKS[h], f"x{h}", keep)
-
-        def quantize_w1(t):
-            return quantize(w1_grouped[:, t, :, :].rearrange("p m j -> p (m j)"), P, f"w1_{t}", keep)
+            nc.vector.tensor_copy(out=target[:, :, u], in_=words.indirect(list_slice(offs_sb, *pieces[h])))
 
         words0 = cast_pairs(0)
-        for h in range(len(PICK_CHUNKS)):
+        for h in range(len(pieces)):
             gather_pairs(words0, 0, h)
         words1 = cast_pairs(1)
-        w1_grouped = deal_weight(w1_raw, "w1")
+
+        w1_first = keep.tile([P, P, PACK], BF16, name="w1_first", tag="after_w1_first", align_bytes=64)
+        w1_rest = keep.tile([P, PACK - 1, P, PACK], BF16, name="w1_rest", align_bytes=64)
+        for q, raw in enumerate(w1_raw):
+            dealt = raw[:].rearrange("p j (m t) -> p m t j", t=PACK)
+            ms = slice(q * (P // 2), (q + 1) * (P // 2))
+            nc.scalar.copy(out=w1_first[:, ms, :], in_=dealt[:, :, 0, :])
+            nc.scalar.copy(out=w1_rest[:, :, ms, :].rearrange("p t m j -> p m t j"), in_=dealt[:, :, 1:, :])
+
+        w1_mx = mx_tiles(H, "w1")
+        x_lo = mx_tiles(HALF, "x_lo")
         gather_pairs(words1, 1, 0)
         gather_pairs(words1, 1, 1)
-        x_mx = [quantize_picked(0)]
+        quantize(x_lo, 0, HALF, picked[0][:].rearrange("p n j -> p (n j)"))
         gather_pairs(words1, 1, 2)
-        x_mx.append(quantize_picked(1))
-        w1_mx = [quantize_w1(0)]
-        x_mx.append(quantize_picked(2))
-        w1_mx.extend([quantize_w1(t) for t in range(1, PACK)])
+        quantize(w1_mx, 0, P, w1_first[:].rearrange("p m j -> p (m j)"))
+        x_hi = mx_tiles(HALF, "x_hi", tag="after_w1_first")
+        quantize(x_hi, 0, QUARTER, picked[1][:].rearrange("p n j -> p (n j)"))
+        quantize(x_hi, QUARTER, QUARTER, picked[2][:].rearrange("p n j -> p (n j)"))
+        for t in range(1, PACK):
+            quantize(w1_mx, t * P, P, w1_rest[:, t - 1, :, :].rearrange("p m j -> p (m j)"))
 
-        def node_product(w_codes, w_scales, name):
+        def node_product(w_mx, t, name, hi_width):
             result = keep.tile([P, S], F32, name=name)
-            for h, width in enumerate(PICK_CHUNKS):
+            runs = [(x_lo, 0, 0, HALF)] + [(x_hi, HALF, n0, hi_width) for n0 in range(0, HALF, hi_width)]
+            for x_mx, base, n0, width in runs:
                 acc = psum.tile([P, width], F32, name="acc", bufs=6)
-                nc.tensor.matmul_mx(
-                    out=acc[:],
-                    lhsT=w_codes.bitcast(FP8X4),
-                    lhsT_scale=w_scales,
-                    rhs=x_mx[h][0][:].bitcast(FP8X4),
-                    rhs_scale=x_mx[h][1][:],
-                    start=True,
-                    stop=True,
-                )
-                nc.scalar.copy(out=result[:, pick_starts[h] : pick_starts[h] + width], in_=acc[:])
+                product(acc, w_mx, t * P, x_mx, n0, width)
+                nc.scalar.copy(out=result[:, base + n0 : base + n0 + width], in_=acc[:])
             return result
 
-        y = [node_product(w1_mx[t][0][:], w1_mx[t][1][:], f"y{t}") for t in range(PACK)]
-        w2_grouped = deal_weight(w2_raw, "w2")
+        w2_grouped = keep.tile([P, PACK, P, PACK], BF16, name="w2_grouped", tag="after_w2", align_bytes=64)
 
-        y_src = [keep.tile([P, U], F32, name=f"y_src{t}") for t in range(PACK)]
+        def deal_w2(q):
+            ms = slice(q * (P // 2), (q + 1) * (P // 2))
+            nc.scalar.copy(
+                out=w2_grouped[:, :, ms, :].rearrange("p t m j -> p m t j"),
+                in_=w2_raw[:].rearrange("p j (m t) -> p m t j", t=PACK)[:, ms, :, :],
+            )
 
-        def gather_sources(t):
-            for h in range(2):
-                nc.vector.tensor_copy(
-                    out=y_src[t][:, h * HALF : (h + 1) * HALF],
-                    in_=y[t][:].indirect(list_slice(src_sb, h * HALF, HALF)),
-                )
+        y = [node_product(w1_mx, 0, "y0", QUARTER), node_product(w1_mx, 1, "y1", HALF)]
+        deal_w2(0)
+        y.append(node_product(w1_mx, 2, "y2", HALF))
+        deal_w2(1)
+        y.append(node_product(w1_mx, 3, "y3", HALF))
 
-        gather_sources(0)
-        gather_sources(1)
-        w2_codes, w2_scales = quantize(w2_grouped[:].rearrange("p t m j -> p (t m j)"), H, "w2", keep)
-        e = [node_product(w2_codes[:, t * P : (t + 1) * P], w2_scales[:, t * P : (t + 1) * P], f"e{t}") for t in range(PACK)]
+        y_src = {}
+
+        def gather_sources(t, h, tag=""):
+            y_src[t, h] = keep.tile([P, HALF], F32, name=f"y_src{t}_{h}", tag=tag, align_bytes=64)
+            nc.vector.tensor_copy(out=y_src[t, h][:], in_=y[t][:].indirect(list_slice(src_sb, h * HALF, HALF)))
+
+        for t, h in ((0, 0), (0, 1), (1, 0), (1, 1), (2, 0)):
+            gather_sources(t, h)
+        w2_mx = mx_tiles(H, "w2")
+        quantize(w2_mx, 0, H, w2_grouped[:].rearrange("p t m j -> p (t m j)"))
+        e = [node_product(w2_mx, t, f"e{t}", HALF) for t in range(PACK)]
         w3_grouped = keep.tile([P, N, PACK], BF16, name="w3_grouped", align_bytes=64)
-        nc.scalar.copy(out=w3_grouped[:], in_=w3_raw[0][:].rearrange("p j c -> p c j"))
-        gather_sources(2)
-        gather_sources(3)
-        w3_codes, w3_scales = quantize(w3_grouped[:].rearrange("p c j -> p (c j)"), N, "w3", keep)
+        nc.scalar.copy(out=w3_grouped[:], in_=w3_raw[:].rearrange("p j c -> p c j"))
+        gather_sources(2, 1, tag="after_w2")
+        gather_sources(3, 0)
+        gather_sources(3, 1)
+        w3_mx = mx_tiles(N, "w3")
+        quantize(w3_mx, 0, N, w3_grouped[:].rearrange("p c j -> p (c j)"))
 
-        def edge_sums(r0, width):
-            sums = ring.tile([P, PACK, width], F32, name="sums")
+        def pin(c):
+            return f"after_z{c}" if 0 <= c < PINNED_CHUNKS else ""
+
+        def edge_sums(c, r0, width):
+            sums = keep.tile([P, PACK, width], F32, name=f"sums{c}", tag=pin(c - 2), align_bytes=64)
+            h, y0 = divmod(r0, HALF)
             for t in range(PACK):
                 nc.vector.tensor_tensor(
-                    sums[:, t, :], e[t][:].indirect(list_slice(dst_sb, r0, width)), y_src[t][:, r0 : r0 + width], ADD
+                    sums[:, t, :], e[t][:].indirect(list_slice(dst_sb, r0, width)), y_src[t, h][:, y0 : y0 + width], ADD
                 )
-            z = ring.tile([P, width, PACK], BF16, name="z", align_bytes=64)
+            z = keep.tile([P, width, PACK], BF16, name=f"z{c}", tag=pin(c), align_bytes=64)
             nc.scalar.activation(z[:], sums[:].rearrange("p t r -> p r t"), RELU)
             return z
 
-        def edge_outputs(z, r0, width):
-            z_codes, z_scales = quantize(z[:].rearrange("p r t -> p (r t)"), width, "z", ring)
+        def edge_outputs(c, z, r0, width):
+            z_mx = mx_tiles(width, f"z{c}")
+            quantize(z_mx, 0, width, z[:].rearrange("p r t -> p (r t)"))
             acc = psum.tile([P, width], F32, name="out_acc", bufs=2)
-            nc.tensor.matmul_mx(
-                out=acc[:],
-                lhsT=w3_codes[:].bitcast(FP8X4),
-                lhsT_scale=w3_scales[:],
-                rhs=z_codes[:].bitcast(FP8X4),
-                rhs_scale=z_scales[:],
-                start=True,
-                stop=True,
-            )
-            result = ring.tile([P, width], F32, name="result")
+            product(acc, w3_mx, 0, z_mx, 0, width)
+            result = keep.tile([P, width], F32, name=f"result{c}")
             nc.scalar.copy(out=result[:], in_=acc[:])
             nc.sync.dma_start(out=out[:, r0 : r0 + width], in_=result[:])
 
         pending = None
         r0 = 0
-        for width in EDGE_CHUNKS:
-            z = edge_sums(r0, width)
+        for c, width in enumerate(EDGE_CHUNKS):
+            z = edge_sums(c, r0, width)
             if pending is not None:
                 edge_outputs(*pending)
-            pending = (z, r0, width)
+            pending = (c, z, r0, width)
             r0 = r0 + width
         edge_outputs(*pending)

@@ -14,16 +14,16 @@ FP8X4 = mybir.dt.float8_e4m3fn_x4
 COPY = mybir.ActivationFunctionType.Copy
 RELU = mybir.ActivationFunctionType.Relu
 ADD = mybir.AluOpType.add
+MAX = mybir.AluOpType.max
 
 P = 128
 PACK = 4
 HALF = 512
 QUARTER = 256
 LIST_ROWS = 16
-NODE_CHUNKS = ((1024, 512, 512), (512, 512, 512, 256, 256))
-SCALAR_CHUNKS = 3
-EDGE_CHUNKS = (256, 256, 256, 128, 128)
-PINNED_CHUNKS = 2
+NODE_CHUNKS = ((1024, 1024), (512, 512, 512, 256, 256))
+SCALAR_COLUMNS = ((0, 384), (512, 512, 512, 0, 0))
+EDGE_CHUNKS = (512, 256, 128, 128)
 
 
 def list_slice(tile, start, count):
@@ -96,10 +96,11 @@ def tile_picked_hub_relu_e_kernel(tc, xT, w1, w2, w3, offs, src, dst, out):
                 raw, c0, width = x_raw[u, c]
                 rounded = pairs[:, c0 : c0 + width, :]
                 values = raw[:].rearrange("p e c -> p c e")
-                if u == 1 and c < SCALAR_CHUNKS:
-                    nc.scalar.activation(rounded, values, COPY)
-                else:
-                    nc.vector.tensor_copy(out=rounded, in_=values)
+                split = SCALAR_COLUMNS[u][c]
+                if split > 0:
+                    nc.scalar.activation(rounded[:, :split, :], values[:, :split, :], COPY)
+                if split < width:
+                    nc.vector.tensor_copy(out=rounded[:, split:, :], in_=values[:, split:, :])
             return pairs[:].rearrange("p t e -> p (t e)").bitcast(U32)
 
         def gather_pairs(words, u, h):
@@ -129,17 +130,15 @@ def tile_picked_hub_relu_e_kernel(tc, xT, w1, w2, w3, offs, src, dst, out):
         x_hi = mx_tiles(HALF, "x_hi", tag="after_w1_first")
         quantize(x_hi, 0, QUARTER, picked[1][:].rearrange("p n j -> p (n j)"))
         quantize(x_hi, QUARTER, QUARTER, picked[2][:].rearrange("p n j -> p (n j)"))
-        for t in range(1, PACK):
-            quantize(w1_mx, t * P, P, w1_rest[:, t - 1, :, :].rearrange("p m j -> p (m j)"))
+        quantize(w1_mx, P, P, w1_rest[:, 0, :, :].rearrange("p m j -> p (m j)"))
+        quantize(w1_mx, 2 * P, 2 * P, w1_rest[:, 1:, :, :].rearrange("p t m j -> p (t m j)"))
 
-        def node_product(w_mx, t, name, hi_width):
-            result = keep.tile([P, S], F32, name=name)
-            runs = [(x_lo, 0, 0, HALF)] + [(x_hi, HALF, n0, hi_width) for n0 in range(0, HALF, hi_width)]
-            for x_mx, base, n0, width in runs:
-                acc = psum.tile([P, width], F32, name="acc", bufs=6)
+        def node_product(w_mx, t, result, width):
+            runs = [(x_mx, base, n0) for x_mx, base in ((x_lo, 0), (x_hi, HALF)) for n0 in range(0, HALF, width)]
+            for x_mx, base, n0 in runs:
+                acc = psum.tile([P, width], F32, name="acc", bufs=8)
                 product(acc, w_mx, t * P, x_mx, n0, width)
                 nc.scalar.copy(out=result[:, base + n0 : base + n0 + width], in_=acc[:])
-            return result
 
         w2_grouped = keep.tile([P, PACK, P, PACK], BF16, name="w2_grouped", tag="after_w2", align_bytes=64)
 
@@ -150,60 +149,82 @@ def tile_picked_hub_relu_e_kernel(tc, xT, w1, w2, w3, offs, src, dst, out):
                 in_=w2_raw[:].rearrange("p j (m t) -> p m t j", t=PACK)[:, ms, :, :],
             )
 
-        y = [node_product(w1_mx, 0, "y0", QUARTER), node_product(w1_mx, 1, "y1", HALF)]
+        y_all = keep.tile([P, PACK * S], F32, name="y_all")
+        y_start = [(PACK - 1 - t) * S for t in range(PACK)]
+        y = [y_all[:, y_start[t] : y_start[t] + S] for t in range(PACK)]
+        node_product(w1_mx, 0, y[0], QUARTER)
+        node_product(w1_mx, 1, y[1], HALF)
         deal_w2(0)
-        y.append(node_product(w1_mx, 2, "y2", HALF))
         deal_w2(1)
-        y.append(node_product(w1_mx, 3, "y3", HALF))
+        node_product(w1_mx, 2, y[2], HALF)
+        node_product(w1_mx, 3, y[3], HALF)
 
         y_src = {}
 
-        def gather_sources(t, h, tag=""):
-            y_src[t, h] = keep.tile([P, HALF], F32, name=f"y_src{t}_{h}", tag=tag, align_bytes=64)
-            nc.vector.tensor_copy(out=y_src[t, h][:], in_=y[t][:].indirect(list_slice(src_sb, h * HALF, HALF)))
+        def gather_sources(t, tag=""):
+            if t in (0, PACK - 1):
+                for h in range(2):
+                    fetched = keep.tile([P, HALF], F32, name=f"y_src{t}_{h}", tag=f"y_src{t}_{h}", align_bytes=64)
+                    nc.vector.tensor_copy(out=fetched[:], in_=y[t].indirect(list_slice(src_sb, h * HALF, HALF)))
+                    y_src[t, h] = fetched[:]
+            else:
+                fetched = keep.tile([P, U], F32, name=f"y_src{t}", tag=tag, align_bytes=64)
+                nc.vector.tensor_copy(out=fetched[:], in_=y_all[:, y_start[t] : y_start[t] + 2 * S].indirect(src_sb[:]))
+                y_src[t, 0], y_src[t, 1] = fetched[:, :HALF], fetched[:, HALF:]
 
-        for t, h in ((0, 0), (0, 1), (1, 0), (1, 1), (2, 0)):
-            gather_sources(t, h)
+        gather_sources(0)
+        gather_sources(1)
         w2_mx = mx_tiles(H, "w2")
         quantize(w2_mx, 0, H, w2_grouped[:].rearrange("p t m j -> p (t m j)"))
-        e = [node_product(w2_mx, t, f"e{t}", HALF) for t in range(PACK)]
+        e = [keep.tile([P, S], F32, name=f"e{t}") for t in range(PACK)]
+        for t in range(PACK):
+            node_product(w2_mx, t, e[t], HALF)
         w3_grouped = keep.tile([P, N, PACK], BF16, name="w3_grouped", align_bytes=64)
         nc.scalar.copy(out=w3_grouped[:], in_=w3_raw[:].rearrange("p j c -> p c j"))
-        gather_sources(2, 1, tag="after_w2")
-        gather_sources(3, 0)
-        gather_sources(3, 1)
+        gather_sources(2, tag="after_w2")
+        gather_sources(3)
         w3_mx = mx_tiles(N, "w3")
         quantize(w3_mx, 0, N, w3_grouped[:].rearrange("p c j -> p (c j)"))
 
-        def pin(c):
-            return f"after_z{c}" if 0 <= c < PINNED_CHUNKS else ""
-
-        def edge_sums(c, r0, width):
-            sums = keep.tile([P, PACK, width], F32, name=f"sums{c}", tag=pin(c - 2), align_bytes=64)
+        def edge_sums(r0, width, tag=""):
+            sums = keep.tile([P, PACK, width], F32, name=f"sums{r0}", tag=tag, align_bytes=64)
             h, y0 = divmod(r0, HALF)
             for t in range(PACK):
                 nc.vector.tensor_tensor(
                     sums[:, t, :], e[t][:].indirect(list_slice(dst_sb, r0, width)), y_src[t, h][:, y0 : y0 + width], ADD
                 )
-            z = keep.tile([P, width, PACK], BF16, name=f"z{c}", tag=pin(c), align_bytes=64)
-            nc.scalar.activation(z[:], sums[:].rearrange("p t r -> p r t"), RELU)
+            return sums[:].rearrange("p t r -> p r t")
+
+        def rectify(sums, r0, tag, on_vector=False):
+            z = keep.tile([P, sums.shape[1], PACK], BF16, name=f"z{r0}", tag=tag, align_bytes=64)
+            if on_vector:
+                nc.vector.tensor_scalar(z[:], sums, 0.0, None, MAX)
+            else:
+                nc.scalar.activation(z[:], sums, RELU)
             return z
 
-        def edge_outputs(c, z, r0, width):
-            z_mx = mx_tiles(width, f"z{c}")
+        def edge_outputs(z, r0, tag="", on_vector=False):
+            width = z.shape[1]
+            z_mx = mx_tiles(width, f"z{r0}", tag)
             quantize(z_mx, 0, width, z[:].rearrange("p r t -> p (r t)"))
-            acc = psum.tile([P, width], F32, name="out_acc", bufs=2)
+            acc = psum.tile([P, width], F32, name="acc", bufs=8)
             product(acc, w3_mx, 0, z_mx, 0, width)
-            result = keep.tile([P, width], F32, name=f"result{c}")
-            nc.scalar.copy(out=result[:], in_=acc[:])
+            result = keep.tile([P, width], F32, name=f"result{r0}")
+            if on_vector:
+                nc.vector.tensor_copy(out=result[:], in_=acc[:])
+            else:
+                nc.scalar.copy(out=result[:], in_=acc[:])
             nc.sync.dma_start(out=out[:, r0 : r0 + width], in_=result[:])
 
-        pending = None
-        r0 = 0
-        for c, width in enumerate(EDGE_CHUNKS):
-            z = edge_sums(c, r0, width)
-            if pending is not None:
-                edge_outputs(*pending)
-            pending = (c, z, r0, width)
-            r0 = r0 + width
-        edge_outputs(*pending)
+        sums = edge_sums(0, 512)
+        z0 = rectify(sums[:, :256, :], 0, "after_z0")
+        z1 = rectify(sums[:, 256:, :], 256, "after_z1")
+        z2 = rectify(edge_sums(512, 256, "y_src3_0"), 512, "after_z2")
+        edge_outputs(z0, 0)
+        z3 = rectify(edge_sums(768, 128, "after_z0"), 768, "after_z3")
+        edge_outputs(z1, 256)
+        sums = edge_sums(896, 128, "after_z1")
+        edge_outputs(z2, 512)
+        z4 = rectify(sums, 896, "after_z2", on_vector=True)
+        edge_outputs(z3, 768)
+        edge_outputs(z4, 896, "after_z3", on_vector=True)

from contextlib import ExitStack

import concourse.mybir as mybir

K, T, S, H, N, U = 512, 2048, 1024, 512, 128, 1024
FLOPS = 2 * (2 * K * H * S + H * N * U)

F32 = mybir.dt.float32
BF16 = mybir.dt.bfloat16
U32 = mybir.dt.uint32
U16 = mybir.dt.uint16
U8 = mybir.dt.uint8
FP8X4 = mybir.dt.float8_e4m3fn_x4
COPY = mybir.ActivationFunctionType.Copy
RELU = mybir.ActivationFunctionType.Relu
ADD = mybir.AluOpType.add
MAX = mybir.AluOpType.max

P = 128
PACK = 4
HALF = 512
QUARTER = 256
LIST_ROWS = 16
NODE_CHUNKS = ((1024, 1024), (512, 512, 512, 256, 256))
SCALAR_COLUMNS = ((0, 384), (512, 512, 512, 0, 0))
EDGE_CHUNKS = (512, 256, 128, 128)


def list_slice(tile, start, count):
    return tile[:, start // LIST_ROWS : (start + count) // LIST_ROWS]


def tile_picked_hub_relu_e_kernel(tc, xT, w1, w2, w3, offs, src, dst, out):
    nc = tc.nc
    with ExitStack() as ctx:
        keep = ctx.enter_context(tc.tile_pool(name="keep", bufs=1))
        psum = ctx.enter_context(tc.psum_pool(name="psum", bufs=1))

        offs_sb = keep.tile([P, S // LIST_ROWS], U16, name="offs_sb")
        src_sb = keep.tile([P, U // LIST_ROWS], U16, name="src_sb")
        dst_sb = keep.tile([P, U // LIST_ROWS], U16, name="dst_sb")

        x_rows = xT.rearrange("(p j) t -> p j t", j=PACK)
        x_raw = {}
        for u in range(2):
            c0 = 0
            for c, width in enumerate(NODE_CHUNKS[u]):
                raw = keep.tile([P, 2, width], F32, name=f"x_raw{u}_{c}")
                nc.sync.dma_start(out=raw[:], in_=x_rows[:, 2 * u : 2 * u + 2, c0 : c0 + width])
                x_raw[u, c] = (raw, c0, width)
                c0 = c0 + width
                if (u, c) == (0, 0):
                    nc.sync.dma_start(offs_sb[:], offs)

        w1_rows = w1.rearrange("(p j) c -> p j c", j=PACK)
        w1_raw = []
        for q in range(2):
            raw = keep.tile([P, PACK, H // 2], F32, name=f"w1_raw{q}")
            nc.sync.dma_start(out=raw[:], in_=w1_rows[:, :, q * (H // 2) : (q + 1) * (H // 2)])
            w1_raw.append(raw)
        nc.sync.dma_start(src_sb[:], src)
        w2_raw = keep.tile([P, PACK, H], F32, name="w2_raw")
        nc.sync.dma_start(out=w2_raw[:], in_=w2.rearrange("(p j) c -> p j c", j=PACK))
        nc.sync.dma_start(dst_sb[:], dst)
        w3_raw = keep.tile([P, PACK, N], F32, name="w3_raw")
        nc.sync.dma_start(out=w3_raw[:], in_=w3.rearrange("(p j) c -> p j c", j=PACK))

        def mx_tiles(width, name, tag=""):
            codes = keep.tile([P, width], U32, name=f"{name}_codes", tag=tag, align_bytes=64)
            scales = keep.tile([P, width], U8, name=f"{name}_scales", align_bytes=64)
            return codes, scales

        def quantize(mx, start, width, grouped):
            codes, scales = mx
            nc.vector.quantize_mx(
                out=codes[:, start : start + width].bitcast(FP8X4), scales=scales[:, start : start + width], in_=grouped
            )

        def product(acc, stationary, m0, moving, n0, width):
            nc.tensor.matmul_mx(
                out=acc[:],
                lhsT=stationary[0][:, m0 : m0 + P].bitcast(FP8X4),
                lhsT_scale=stationary[1][:, m0 : m0 + P],
                rhs=moving[0][:, n0 : n0 + width].bitcast(FP8X4),
                rhs_scale=moving[1][:, n0 : n0 + width],
                start=True,
                stop=True,
            )

        pieces = ((0, HALF), (HALF, QUARTER), (HALF + QUARTER, QUARTER))
        picked = [keep.tile([P, width, PACK], BF16, name=f"picked{h}", align_bytes=64) for h, (s0, width) in enumerate(pieces)]

        def cast_pairs(u):
            pairs = keep.tile([P, T, 2], BF16, name=f"pairs{u}", align_bytes=64)
            for c in range(len(NODE_CHUNKS[u])):
                raw, c0, width = x_raw[u, c]
                rounded = pairs[:, c0 : c0 + width, :]
                values = raw[:].rearrange("p e c -> p c e")
                split = SCALAR_COLUMNS[u][c]
                if split > 0:
                    nc.scalar.activation(rounded[:, :split, :], values[:, :split, :], COPY)
                if split < width:
                    nc.vector.tensor_copy(out=rounded[:, split:, :], in_=values[:, split:, :])
            return pairs[:].rearrange("p t e -> p (t e)").bitcast(U32)

        def gather_pairs(words, u, h):
            target = picked[h][:].rearrange("p n j -> p (n j)").bitcast(U32).rearrange("p (n u) -> p n u", u=2)
            nc.vector.tensor_copy(out=target[:, :, u], in_=words.indirect(list_slice(offs_sb, *pieces[h])))

        words0 = cast_pairs(0)
        for h in range(len(pieces)):
            gather_pairs(words0, 0, h)
        words1 = cast_pairs(1)

        w1_first = keep.tile([P, P, PACK], BF16, name="w1_first", tag="after_w1_first", align_bytes=64)
        w1_rest = keep.tile([P, PACK - 1, P, PACK], BF16, name="w1_rest", align_bytes=64)
        for q, raw in enumerate(w1_raw):
            dealt = raw[:].rearrange("p j (m t) -> p m t j", t=PACK)
            ms = slice(q * (P // 2), (q + 1) * (P // 2))
            nc.scalar.copy(out=w1_first[:, ms, :], in_=dealt[:, :, 0, :])
            nc.scalar.copy(out=w1_rest[:, :, ms, :].rearrange("p t m j -> p m t j"), in_=dealt[:, :, 1:, :])

        w1_mx = mx_tiles(H, "w1")
        x_lo = mx_tiles(HALF, "x_lo")
        gather_pairs(words1, 1, 0)
        gather_pairs(words1, 1, 1)
        quantize(x_lo, 0, HALF, picked[0][:].rearrange("p n j -> p (n j)"))
        gather_pairs(words1, 1, 2)
        quantize(w1_mx, 0, P, w1_first[:].rearrange("p m j -> p (m j)"))
        x_hi = mx_tiles(HALF, "x_hi", tag="after_w1_first")
        quantize(x_hi, 0, QUARTER, picked[1][:].rearrange("p n j -> p (n j)"))
        quantize(x_hi, QUARTER, QUARTER, picked[2][:].rearrange("p n j -> p (n j)"))
        quantize(w1_mx, P, P, w1_rest[:, 0, :, :].rearrange("p m j -> p (m j)"))
        quantize(w1_mx, 2 * P, 2 * P, w1_rest[:, 1:, :, :].rearrange("p t m j -> p (t m j)"))

        def node_product(w_mx, t, result, width):
            runs = [(x_mx, base, n0) for x_mx, base in ((x_lo, 0), (x_hi, HALF)) for n0 in range(0, HALF, width)]
            for x_mx, base, n0 in runs:
                acc = psum.tile([P, width], F32, name="acc", bufs=8)
                product(acc, w_mx, t * P, x_mx, n0, width)
                nc.scalar.copy(out=result[:, base + n0 : base + n0 + width], in_=acc[:])

        w2_grouped = keep.tile([P, PACK, P, PACK], BF16, name="w2_grouped", tag="after_w2", align_bytes=64)

        def deal_w2(q):
            ms = slice(q * (P // 2), (q + 1) * (P // 2))
            nc.scalar.copy(
                out=w2_grouped[:, :, ms, :].rearrange("p t m j -> p m t j"),
                in_=w2_raw[:].rearrange("p j (m t) -> p m t j", t=PACK)[:, ms, :, :],
            )

        y_all = keep.tile([P, PACK * S], F32, name="y_all")
        y_start = [(PACK - 1 - t) * S for t in range(PACK)]
        y = [y_all[:, y_start[t] : y_start[t] + S] for t in range(PACK)]
        node_product(w1_mx, 0, y[0], QUARTER)
        node_product(w1_mx, 1, y[1], HALF)
        deal_w2(0)
        deal_w2(1)
        node_product(w1_mx, 2, y[2], HALF)
        node_product(w1_mx, 3, y[3], HALF)

        y_src = {}

        def gather_sources(t, tag=""):
            if t in (0, PACK - 1):
                for h in range(2):
                    fetched = keep.tile([P, HALF], F32, name=f"y_src{t}_{h}", tag=f"y_src{t}_{h}", align_bytes=64)
                    nc.vector.tensor_copy(out=fetched[:], in_=y[t].indirect(list_slice(src_sb, h * HALF, HALF)))
                    y_src[t, h] = fetched[:]
            else:
                fetched = keep.tile([P, U], F32, name=f"y_src{t}", tag=tag, align_bytes=64)
                nc.vector.tensor_copy(out=fetched[:], in_=y_all[:, y_start[t] : y_start[t] + 2 * S].indirect(src_sb[:]))
                y_src[t, 0], y_src[t, 1] = fetched[:, :HALF], fetched[:, HALF:]

        gather_sources(0)
        gather_sources(1)
        w2_mx = mx_tiles(H, "w2")
        quantize(w2_mx, 0, H, w2_grouped[:].rearrange("p t m j -> p (t m j)"))
        e = [keep.tile([P, S], F32, name=f"e{t}") for t in range(PACK)]
        for t in range(PACK):
            node_product(w2_mx, t, e[t], HALF)
        w3_grouped = keep.tile([P, N, PACK], BF16, name="w3_grouped", align_bytes=64)
        nc.scalar.copy(out=w3_grouped[:], in_=w3_raw[:].rearrange("p j c -> p c j"))
        gather_sources(2, tag="after_w2")
        gather_sources(3)
        w3_mx = mx_tiles(N, "w3")
        quantize(w3_mx, 0, N, w3_grouped[:].rearrange("p c j -> p (c j)"))

        def edge_sums(r0, width, tag=""):
            sums = keep.tile([P, PACK, width], F32, name=f"sums{r0}", tag=tag, align_bytes=64)
            h, y0 = divmod(r0, HALF)
            for t in range(PACK):
                nc.vector.tensor_tensor(
                    sums[:, t, :], e[t][:].indirect(list_slice(dst_sb, r0, width)), y_src[t, h][:, y0 : y0 + width], ADD
                )
            return sums[:].rearrange("p t r -> p r t")

        def rectify(sums, r0, tag, on_vector=False):
            z = keep.tile([P, sums.shape[1], PACK], BF16, name=f"z{r0}", tag=tag, align_bytes=64)
            if on_vector:
                nc.vector.tensor_scalar(z[:], sums, 0.0, None, MAX)
            else:
                nc.scalar.activation(z[:], sums, RELU)
            return z

        def edge_outputs(z, r0, tag="", on_vector=False):
            width = z.shape[1]
            z_mx = mx_tiles(width, f"z{r0}", tag)
            quantize(z_mx, 0, width, z[:].rearrange("p r t -> p (r t)"))
            acc = psum.tile([P, width], F32, name="acc", bufs=8)
            product(acc, w3_mx, 0, z_mx, 0, width)
            result = keep.tile([P, width], F32, name=f"result{r0}")
            if on_vector:
                nc.vector.tensor_copy(out=result[:], in_=acc[:])
            else:
                nc.scalar.copy(out=result[:], in_=acc[:])
            nc.sync.dma_start(out=out[:, r0 : r0 + width], in_=result[:])

        sums = edge_sums(0, 512)
        z0 = rectify(sums[:, :256, :], 0, "after_z0")
        z1 = rectify(sums[:, 256:, :], 256, "after_z1")
        z2 = rectify(edge_sums(512, 256, "y_src3_0"), 512, "after_z2")
        edge_outputs(z0, 0)
        z3 = rectify(edge_sums(768, 128, "after_z0"), 768, "after_z3")
        edge_outputs(z1, 256)
        sums = edge_sums(896, 128, "after_z1")
        edge_outputs(z2, 512)
        z4 = rectify(sums, 896, "after_z2", on_vector=True)
        edge_outputs(z3, 768)
        edge_outputs(z4, 896, "after_z3", on_vector=True)
